import numpy as np
import ml_dtypes


def mxq(x, axis, fmt="e4m3"):
    dtype, down = {"e4m3": (ml_dtypes.float8_e4m3fn, 7), "e5m2": (ml_dtypes.float8_e5m2, 14)}[fmt]
    v = np.moveaxis(np.asarray(x, np.float32).astype(ml_dtypes.bfloat16).astype(np.float64), axis, -1)
    blocks = v.reshape(v.shape[:-1] + (-1, 32))
    amax = np.abs(blocks).max(-1, keepdims=True)
    byte = np.maximum(np.where(amax > 0, np.frexp(amax)[1] - 1 + 127, 0) - down, 1)
    scale = np.exp2(byte - 127.0)
    codes = (blocks / scale).astype(np.float32).astype(dtype).astype(np.float64)
    return np.moveaxis((codes * scale).reshape(v.shape), -1, axis)


WIDE = False


def mx_kscale(k):
    if not WIDE:
        return np.ones(k)
    levels = np.array([10, -10, 5, -5, 0])
    if k % 512:
        return np.exp2(np.random.permutation(np.resize(levels, k // 32))).repeat(32)
    a = np.empty((k // 512, 16))
    for p in range(k // 512):
        a[p, :8] = np.random.permutation(np.resize(levels, 8))
        for g in range(8):
            far = levels[np.abs(levels - a[p, g]) >= 10]
            a[p, g + 8] = far[np.random.randint(len(far))]
    return np.exp2(a.ravel()).repeat(32)


def f64(x):
    return np.asarray(x).astype(np.float64)


E2M1 = np.array([0.0, 0.5, 1.0, 1.5, 2.0, 3.0, 4.0, 6.0, -0.0, -0.5, -1.0, -1.5, -2.0, -3.0, -4.0, -6.0])


def pack_weight(w, fmt):
    k, n = w.shape
    w = f64(np.asarray(w, np.float32).astype(ml_dtypes.bfloat16)).reshape(k // 32, 32, n)
    amax = np.abs(w).max(1)
    if fmt == "e4m3":
        byte = np.frexp(amax)[1] - 1 + 127 - 7
    else:
        mant, ex = np.frexp(amax / 6.0)
        byte = np.where(mant > 0.5, ex, ex - 1) + 127
    byte = np.clip(np.where(amax > 0, byte, 1), 1, 254)
    scaled = (w * np.exp2(127.0 - byte)[:, None, :]).reshape(k, n).astype(np.float32)
    by_word = np.ascontiguousarray(scaled.reshape(k // 512, 128, 4, n).transpose(0, 1, 3, 2))
    if fmt == "e4m3":
        words = by_word.astype(ml_dtypes.float8_e4m3fn).view(np.uint8)
    else:
        c = by_word.astype(ml_dtypes.float4_e2m1fn).view(np.uint8) & 0xF
        words = (c[..., 0::2] | (c[..., 1::2] << 4)).reshape(k // 512, 128, 2 * n)
    return np.ascontiguousarray(words), np.ascontiguousarray(byte.astype(np.uint8).reshape(k // 512, 16, n))


def unpack_weight(words, scales, fmt):
    g, _, n = scales.shape
    words = np.ascontiguousarray(words).reshape(g, 128, n, -1)
    if fmt == "e4m3":
        vals = words.view(ml_dtypes.float8_e4m3fn).astype(np.float64)
    else:
        nib = np.empty((g, 128, n, 4), np.uint8)
        nib[..., 0::2] = words & 0xF
        nib[..., 1::2] = words >> 4
        vals = E2M1[nib]
    vals = vals * np.repeat(np.exp2(scales.astype(np.float64) - 127.0), 8, axis=1)[..., None]
    return vals.transpose(0, 1, 3, 2).reshape(g * 512, n)


def bf(x):
    return np.asarray(x, np.float32).astype(ml_dtypes.bfloat16)


def planes(Y):
    r, m = Y.shape
    b = f64(bf(Y)).reshape(r // 32, 32, m)
    amax = np.abs(b).max(1)
    byte = np.clip(np.where(amax > 0, np.frexp(amax)[1] - 1 + 127 - 7, 1), 1, 254)
    codes = (b * np.exp2(127.0 - byte)[:, None, :]).reshape(r, m).astype(np.float32).astype(ml_dtypes.float8_e4m3fn).view(np.uint8)
    words = codes.reshape(r // 512, 128, 4, m).transpose(0, 1, 3, 2)
    return np.ascontiguousarray(words), np.ascontiguousarray(byte.astype(np.uint8).reshape(r // 512, 16, m))


K, T, J, N = 1024, 512, 512, 512


def setup_inputs():
    n = np.random.standard_normal
    fk = mx_kscale(K)
    fj = mx_kscale(J)
    xtp = pack_weight(n((K, T)) * 0.4 / fk[:, None], "e2m1")
    wsp = pack_weight(n((K, J)) * 1 / np.sqrt(K) * fk[:, None], "e4m3")
    wop = pack_weight(n((J, N)) * 1 / np.sqrt(J) / fj[:, None], "e2m1")
    wyp = pack_weight(n((K, N)) * 2.0 / np.sqrt(K) * fk[:, None], "e4m3")
    return {
        "xt_words": xtp[0],
        "xt_scales": xtp[1],
        "ws_words": wsp[0],
        "ws_scales": wsp[1],
        "fj": (np.random.uniform(64.0, 128.0, (J, 1)) * fj[:, None]).astype(np.float32),
        "wo_words": wop[0],
        "wo_scales": wop[1],
        "wy_words": wyp[0],
        "wy_scales": wyp[1],
    }


def reference(xt_words, xt_scales, ws_words, ws_scales, fj, wo_words, wo_scales, wy_words, wy_scales):
    xtu = unpack_weight(xt_words, xt_scales, "e2m1")
    wsu = unpack_weight(ws_words, ws_scales, "e4m3")
    wou = unpack_weight(wo_words, wo_scales, "e2m1")
    wyu = unpack_weight(wy_words, wy_scales, "e4m3")
    a = xtu.T @ wsu
    e = np.exp(a)
    q = e / np.sum(e, axis=1, keepdims=True)
    qt = q.T
    qw = qt * f64(fj)
    qwq = mxq(qw, 0, "e4m3")
    y = wou.T @ qwq + wyu.T @ xtu
    words, scales = planes(y)
    return y, words, scales

@@ -1,0 +1,282 @@
+from contextlib import ExitStack
+
+import concourse.mybir as mybir
+from concourse.masks import make_identity
+
+K, T, J, N = 1024, 512, 512, 512
+FLOPS = 2 * K * T * J + 2 * J * N * T + 2 * K * N * T
+
+F32 = mybir.dt.float32
+BF16 = mybir.dt.bfloat16
+I32 = mybir.dt.int32
+U32 = mybir.dt.uint32
+U8 = mybir.dt.uint8
+FP8X4 = mybir.dt.float8_e4m3fn_x4
+FP4X4 = mybir.dt.float4_e2m1fn_x4
+ALU = mybir.AluOpType
+ACT = mybir.ActivationFunctionType
+AX = mybir.AxisListType
+
+P = 128
+PACK = 4
+PASSES = K // (P * PACK)
+TILES = T // P
+QUADS = 4
+
+
+def tile_mix_shares_carry_slot_rows_pl_kernel(
+    tc, xt_words, xt_scales, ws_words, ws_scales, fj, wo_words, wo_scales, wy_words, wy_scales,
+    out_0, out_1, out_2,
+):
+    nc = tc.nc
+    with ExitStack() as ctx:
+        sb = ctx.enter_context(tc.tile_pool(name="sb", bufs=1))
+        ps = ctx.enter_context(tc.psum_pool(name="ps", bufs=1))
+        ctx.enter_context(tc.manual_schedule())
+
+        def sbuf(name, shape, dtype):
+            return sb.tile(shape, dtype, name=name, align_bytes=64)
+
+        def bank(number, name, shape):
+            return ps.tile(shape, F32, name=name, tag="bank%d" % number)
+
+        x_w = sbuf("x_w", [P, PASSES, 2 * T], U8)
+        x_s = sbuf("x_s", [P, PASSES, T], U8)
+        ws_w = sbuf("ws_w", [P, PASSES, J], I32)
+        ws_s = sbuf("ws_s", [P, PASSES, J], U8)
+        wy_w_in = sbuf("wy_w_in", [P, PASSES, N], I32)
+        wy_s_in = sbuf("wy_s_in", [P, PASSES, N], U8)
+        wo_w_in = sbuf("wo_w_in", [P, 2 * N], U8)
+        wo_s_in = sbuf("wo_s_in", [P, 1, N], U8)
+        wy_w = [sbuf("wy_w%d" % z, [P, PACK, P], I32) for z in range(PASSES)]
+        wy_s = sbuf("wy_s", [P, PASSES, PACK, P], U8)
+        wo_w = sbuf("wo_w", [P, PACK, 2 * P], U8)
+        wo_s = sbuf("wo_s", [P, PACK, P], U8)
+        fj_col = sbuf("fj_col", [P, PACK], F32)
+        ident = sbuf("ident", [P, P], F32)
+        y_scales = sbuf("y_scales", [P, T], U8)
+
+        def load_scale_rows(engine, plane, rows, q):
+            engine.dma_start(
+                out=plane[32 * q : 32 * q + 4].bitcast(I32),
+                in_=rows[:, 4 * q : 4 * q + 4, :].rearrange("z r c -> r z c").bitcast(I32),
+            )
+
+        nc.gpsimd.memset(x_s[:].bitcast(I32), 0)
+        nc.vector.memset(ws_s[:].bitcast(I32), 0)
+        nc.gpsimd.memset(wy_s_in[:].bitcast(I32), 0)
+        nc.vector.memset(wo_s_in[:].bitcast(I32), 0)
+        make_identity(nc, ident[:])
+
+        for q in range(2):
+            load_scale_rows(nc.sync, x_s, xt_scales, q)
+        nc.sync.dma_start(out=x_w[:].bitcast(I32), in_=xt_words.rearrange("z p c -> p z c").bitcast(I32))
+        nc.sync.dma_start(out=ws_w[:], in_=ws_words.rearrange("z p c r -> p z (c r)").bitcast(I32))
+        for q in range(2, QUADS):
+            load_scale_rows(nc.sync, x_s, xt_scales, q)
+        for q in range(QUADS):
+            load_scale_rows(nc.sync, ws_s, ws_scales, q)
+        nc.sync.dma_start(out=wy_w_in[:], in_=wy_words.rearrange("z p c r -> p z (c r)").bitcast(I32))
+        nc.sync.dma_start(out=fj_col[:], in_=fj.rearrange("(p r) o -> p (r o)", r=PACK))
+        for q in range(QUADS):
+            load_scale_rows(nc.sync, wy_s_in, wy_scales, q)
+        nc.sync.dma_start(out=wo_w_in[:].bitcast(I32), in_=wo_words[0].bitcast(I32))
+        for q in range(QUADS):
+            load_scale_rows(nc.sync, wo_s_in, wo_scales, q)
+
+        def x_codes(z, i):
+            return x_w[:, z, 2 * P * i : 2 * P * (i + 1)].bitcast(FP4X4)
+
+        def x_plane(z, i):
+            return x_s[:, z, P * i : P * (i + 1)]
+
+        score, neg_max, e, total, inv, qw, turned, grouped, q_codes, q_plane = ({} for n in range(10))
+        y, y_f32, y_bf = {}, {}, {}
+
+        def scores(i):
+            score[i] = bank(i, "score%d" % i, [P, J])
+            for z in range(PASSES):
+                nc.tensor.matmul_mx(
+                    out=score[i][:], lhsT=x_codes(z, i), lhsT_scale=x_plane(z, i),
+                    rhs=ws_w[:, z, :].bitcast(FP8X4), rhs_scale=ws_s[:, z, :],
+                    start=(z == 0), stop=(z == PASSES - 1),
+                )
+
+        fj_rows = bank(7, "fj_rows", [P, 2, P, 2])
+
+        def spread_fj():
+            for r in range(PACK):
+                nc.tensor.transpose(
+                    fj_rows[:, r // 2, :, r % 2], fj_col[:, r : r + 1].to_broadcast([P, P]), ident[:]
+                )
+
+        def row_max(i):
+            neg_max[i] = sbuf("neg_max%d" % i, [P, 1], F32)
+            nc.vector.tensor_reduce(out=neg_max[i][:], in_=score[i][:], axis=AX.X, op=ALU.max, negate=True)
+
+        def exponentials(i):
+            e[i] = sbuf("e%d" % i, [P, 2, P, 2], F32)
+            total[i] = sbuf("total%d" % i, [P, 1], F32)
+            nc.scalar.activation(
+                out=e[i][:], in_=score[i][:].rearrange("p (m u v) -> p u m v", u=2, v=2),
+                func=ACT.Exp, bias=neg_max[i][:], scale=1.0, accum_out=total[i][:],
+            )
+
+        def reciprocal(i):
+            inv[i] = sbuf("inv%d" % i, [P, 1], F32)
+            nc.vector.reciprocal(out=inv[i][:], in_=total[i][:])
+
+        def weigh(i):
+            qw[i] = sbuf("qw%d" % i, [P, J], BF16)
+            nc.vector.scalar_tensor_tensor(
+                out=qw[i][:], in0=e[i][:].rearrange("p u m v -> p (u m v)"), scalar=inv[i][:],
+                in1=fj_rows[:].rearrange("p u m v -> p (u m v)"), op0=ALU.mult, op1=ALU.mult,
+            )
+
+        def turn(i):
+            turned[i] = bank(i % 2, "turned%d" % i, [P, 2, P])
+            pairs = qw[i][:].bitcast(F32)
+            for u in range(2):
+                nc.tensor.transpose(turned[i][:, u, :], pairs[:, P * u : P * (u + 1)], ident[:])
+
+        def group(i):
+            grouped[i] = sbuf("grouped%d" % i, [P, PACK * P], BF16)
+            nc.scalar.copy(
+                out=grouped[i][:].bitcast(F32).rearrange("p (t u) -> p t u", u=2),
+                in_=turned[i][:].rearrange("p u t -> p t u"),
+            )
+
+        def quantise_shares(i):
+            q_codes[i] = sbuf("q_codes%d" % i, [P, P], U32)
+            q_plane[i] = sbuf("q_plane%d" % i, [P, P], U8)
+            nc.vector.quantize_mx(out=q_codes[i][:].bitcast(FP8X4), scales=q_plane[i][:], in_=grouped[i][:])
+
+        def deal_wy_words(z):
+            nc.vector.tensor_copy(
+                out=wy_w[z][:].rearrange("p r (b m) -> p b r m", m=4),
+                in_=wy_w_in[:, z, :].rearrange("p (b m r) -> p b r m", m=4, r=PACK),
+            )
+
+        def deal_wy_scales():
+            nc.gpsimd.tensor_copy(out=wy_s[:], in_=wy_s_in[:].rearrange("p z (m r) -> p z r m", r=PACK))
+
+        def deal_wo_words():
+            nc.gpsimd.tensor_copy(
+                out=wo_w[:].rearrange("p r (b m h) -> p b r m h", m=8, h=2),
+                in_=wo_w_in[:].rearrange("p (b m r h) -> p b r m h", m=8, r=PACK, h=2),
+            )
+
+        def deal_wo_scales():
+            nc.vector.tensor_copy(out=wo_s[:], in_=wo_s_in[:, 0, :].rearrange("p (m r) -> p r m", r=PACK))
+
+        def own_product(i):
+            y[i] = bank((4, 5, 6, 2)[i], "y%d" % i, [P, PACK, P])
+            for z in range(PASSES):
+                for r in range(PACK):
+                    nc.tensor.matmul_mx(
+                        out=y[i][:, r, :], lhsT=wy_w[z][:, r, :].bitcast(FP8X4), lhsT_scale=wy_s[:, z, r, :],
+                        rhs=x_codes(z, i), rhs_scale=x_plane(z, i),
+                        start=(z == 0 and r == 0), stop=False,
+                    )
+
+        def carry(i):
+            for r in range(PACK):
+                nc.tensor.matmul_mx(
+                    out=y[i][:, r, :], lhsT=wo_w[:, r, :].bitcast(FP4X4), lhsT_scale=wo_s[:, r, :],
+                    rhs=q_codes[i][:].bitcast(FP8X4), rhs_scale=q_plane[i][:],
+                    start=False, stop=(r == PACK - 1),
+                )
+
+        def hand_out_values(i, copy):
+            y_f32[i] = sbuf("y_f32_%d" % i, [P, PACK, P], F32)
+            copy(out=y_f32[i][:], in_=y[i][:])
+            nc.sync.dma_start(
+                out=out_0.rearrange("(p r) t -> p r t", r=PACK)[:, :, P * i : P * (i + 1)], in_=y_f32[i][:]
+            )
+
+        def round_on_scalar(i):
+            y_bf[i] = sbuf("y_bf%d" % i, [P, P, PACK], BF16)
+            nc.scalar.copy(out=y_bf[i][:], in_=y[i][:].rearrange("p r t -> p t r"))
+
+        def round_on_vector(i):
+            y_bf[i] = sbuf("y_bf%d" % i, [P, P, PACK], BF16)
+            nc.vector.tensor_copy(
+                out=y_bf[i][:].rearrange("p (c m) r -> p c r m", m=4),
+                in_=y_f32[i][:].rearrange("p r (c m) -> p c r m", m=4),
+            )
+
+        def hand_out_codes(i):
+            y_codes = sbuf("y_codes%d" % i, [P, P], U32)
+            nc.vector.quantize_mx(
+                out=y_codes[:].bitcast(FP8X4), scales=y_scales[:, P * i : P * (i + 1)],
+                in_=y_bf[i][:].rearrange("p t r -> p (t r)"),
+            )
+            nc.sync.dma_start(
+                out=out_1[0].rearrange("p c r -> p (c r)").bitcast(I32)[:, P * i : P * (i + 1)],
+                in_=y_codes[:].bitcast(I32),
+            )
+
+        scores(0)
+        scores(1)
+        spread_fj()
+        scores(2)
+        scores(3)
+        deal_wy_scales()
+        deal_wo_words()
+        row_max(0)
+        exponentials(0)
+        deal_wy_words(0)
+        deal_wy_words(1)
+        row_max(1)
+        exponentials(1)
+        reciprocal(0)
+        row_max(2)
+        exponentials(2)
+        weigh(0)
+        turn(0)
+        group(0)
+        own_product(0)
+        reciprocal(1)
+        row_max(3)
+        exponentials(3)
+        weigh(1)
+        turn(1)
+        group(1)
+        own_product(1)
+        reciprocal(2)
+        deal_wo_scales()
+        quantise_shares(0)
+        carry(0)
+        weigh(2)
+        turn(2)
+        own_product(2)
+        reciprocal(3)
+        quantise_shares(1)
+        carry(1)
+        hand_out_values(0, nc.scalar.copy)
+        group(2)
+        weigh(3)
+        turn(3)
+        own_product(3)
+        quantise_shares(2)
+        carry(2)
+        round_on_scalar(0)
+        group(3)
+        hand_out_values(1, nc.vector.tensor_copy)
+        hand_out_codes(0)
+        quantise_shares(3)
+        carry(3)
+        hand_out_values(2, nc.scalar.copy)
+        round_on_vector(1)
+        hand_out_values(3, nc.scalar.copy)
+        round_on_vector(2)
+        hand_out_codes(1)
+        hand_out_codes(2)
+        round_on_vector(3)
+        hand_out_codes(3)
+        for q in range(QUADS):
+            engine = nc.sync if q % 2 else nc.scalar
+            engine.dma_start(
+                out=out_2[0, 4 * q : 4 * q + 4, :].bitcast(I32),
+                in_=y_scales[32 * q : 32 * q + 4, :].bitcast(I32),
+            )

@@ -55,6 +55,7 @@ def tile_mix_shares_carry_slot_rows_pl_kernel(
         fj_col = sbuf("fj_col", [P, PACK], F32)
         ident = sbuf("ident", [P, P], F32)
         y_scales = sbuf("y_scales", [P, T], U8)
+        y_codes = sbuf("y_codes", [P, T], U32)
 
         def load_scale_rows(engine, plane, rows, q):
             engine.dma_start(
@@ -158,10 +159,10 @@ def tile_mix_shares_carry_slot_rows_pl_kernel(
             )
 
         def deal_wy_scales():
-            nc.gpsimd.tensor_copy(out=wy_s[:], in_=wy_s_in[:].rearrange("p z (m r) -> p z r m", r=PACK))
+            nc.vector.tensor_copy(out=wy_s[:], in_=wy_s_in[:].rearrange("p z (m r) -> p z r m", r=PACK))
 
         def deal_wo_words():
-            nc.gpsimd.tensor_copy(
+            nc.vector.tensor_copy(
                 out=wo_w[:].rearrange("p r (b m h) -> p b r m h", m=8, h=2),
                 in_=wo_w_in[:].rearrange("p (b m r h) -> p b r m h", m=8, r=PACK, h=2),
             )
@@ -194,10 +195,6 @@ def tile_mix_shares_carry_slot_rows_pl_kernel(
                 out=out_0.rearrange("(p r) t -> p r t", r=PACK)[:, :, P * i : P * (i + 1)], in_=y_f32[i][:]
             )
 
-        def round_on_scalar(i):
-            y_bf[i] = sbuf("y_bf%d" % i, [P, P, PACK], BF16)
-            nc.scalar.copy(out=y_bf[i][:], in_=y[i][:].rearrange("p r t -> p t r"))
-
         def round_on_vector(i):
             y_bf[i] = sbuf("y_bf%d" % i, [P, P, PACK], BF16)
             nc.vector.tensor_copy(
@@ -206,73 +203,74 @@ def tile_mix_shares_carry_slot_rows_pl_kernel(
             )
 
         def hand_out_codes(i):
-            y_codes = sbuf("y_codes%d" % i, [P, P], U32)
             nc.vector.quantize_mx(
-                out=y_codes[:].bitcast(FP8X4), scales=y_scales[:, P * i : P * (i + 1)],
+                out=y_codes[:, P * i : P * (i + 1)].bitcast(FP8X4), scales=y_scales[:, P * i : P * (i + 1)],
                 in_=y_bf[i][:].rearrange("p t r -> p (t r)"),
             )
-            nc.sync.dma_start(
-                out=out_1[0].rearrange("p c r -> p (c r)").bitcast(I32)[:, P * i : P * (i + 1)],
-                in_=y_codes[:].bitcast(I32),
-            )
+            if i % 2:
+                both = slice(P * (i - 1), P * (i + 1))
+                nc.sync.dma_start(
+                    out=out_1[0].rearrange("p c r -> p (c r)").bitcast(I32)[:, both],
+                    in_=y_codes[:, both].bitcast(I32),
+                )
 
         scores(0)
         scores(1)
-        spread_fj()
         scores(2)
+        spread_fj()
         scores(3)
-        deal_wy_scales()
-        deal_wo_words()
+        deal_wy_words(0)
         row_max(0)
         exponentials(0)
-        deal_wy_words(0)
         deal_wy_words(1)
         row_max(1)
         exponentials(1)
+        deal_wy_scales()
+        own_product(0)
+        own_product(1)
         reciprocal(0)
         row_max(2)
         exponentials(2)
         weigh(0)
         turn(0)
-        group(0)
-        own_product(0)
+        own_product(2)
         reciprocal(1)
         row_max(3)
         exponentials(3)
+        group(0)
         weigh(1)
         turn(1)
         group(1)
-        own_product(1)
+        own_product(3)
         reciprocal(2)
         deal_wo_scales()
-        quantise_shares(0)
-        carry(0)
         weigh(2)
         turn(2)
-        own_product(2)
-        reciprocal(3)
-        quantise_shares(1)
-        carry(1)
-        hand_out_values(0, nc.scalar.copy)
         group(2)
+        reciprocal(3)
+        quantise_shares(0)
         weigh(3)
         turn(3)
-        own_product(3)
+        group(3)
+        deal_wo_words()
+        carry(0)
+        quantise_shares(1)
+        carry(1)
         quantise_shares(2)
         carry(2)
-        round_on_scalar(0)
-        group(3)
-        hand_out_values(1, nc.vector.tensor_copy)
-        hand_out_codes(0)
+        hand_out_values(0, nc.scalar.copy)
         quantise_shares(3)
         carry(3)
+        hand_out_values(1, nc.vector.tensor_copy)
         hand_out_values(2, nc.scalar.copy)
+        round_on_vector(0)
         round_on_vector(1)
         hand_out_values(3, nc.scalar.copy)
+        hand_out_codes(0)
         round_on_vector(2)
         hand_out_codes(1)
-        hand_out_codes(2)
         round_on_vector(3)
+        hand_out_codes(2)
         hand_out_codes(3)
         for q in range(QUADS):
             engine = nc.sync if q % 2 else nc.scalar

@@ -22,6 +22,7 @@ PACK = 4
 PASSES = K // (P * PACK)
 TILES = T // P
 QUADS = 4
+WARM_UP_PASSES = 12
 
 
 def tile_mix_shares_carry_slot_rows_pl_kernel(
@@ -48,8 +49,8 @@ def tile_mix_shares_carry_slot_rows_pl_kernel(
         wy_s_in = sbuf("wy_s_in", [P, PASSES, N], U8)
         wo_w_in = sbuf("wo_w_in", [P, 2 * N], U8)
         wo_s_in = sbuf("wo_s_in", [P, 1, N], U8)
-        wy_w = [sbuf("wy_w%d" % z, [P, PACK, P], I32) for z in range(PASSES)]
-        wy_s = sbuf("wy_s", [P, PASSES, PACK, P], U8)
+        wy_w = sbuf("wy_w", [P, PASSES, PACK, P], I32)
+        wy_s = [sbuf("wy_s%d" % z, [P, PACK, P], U8) for z in range(PASSES)]
         wo_w = sbuf("wo_w", [P, PACK, 2 * P], U8)
         wo_s = sbuf("wo_s", [P, PACK, P], U8)
         fj_col = sbuf("fj_col", [P, PACK], F32)
@@ -64,21 +65,23 @@ def tile_mix_shares_carry_slot_rows_pl_kernel(
             )
 
         nc.gpsimd.memset(x_s[:].bitcast(I32), 0)
-        nc.vector.memset(ws_s[:].bitcast(I32), 0)
-        nc.gpsimd.memset(wy_s_in[:].bitcast(I32), 0)
-        nc.vector.memset(wo_s_in[:].bitcast(I32), 0)
         make_identity(nc, ident[:])
+        zeros = sbuf("zeros", [P, PACK * P], BF16)
+        zero_codes = sbuf("zero_codes", [P, P], U32)
+        zero_plane = sbuf("zero_plane", [P, P], U8)
+        for blank in (ws_s, zeros, wy_s_in, wo_s_in):
+            nc.vector.memset(blank[:].bitcast(I32), 0)
+        nc.vector.quantize_mx(out=zero_codes[:].bitcast(FP8X4), scales=zero_plane[:], in_=zeros[:])
 
-        for q in range(2):
-            load_scale_rows(nc.sync, x_s, xt_scales, q)
+        nc.sync.dma_start(out=fj_col[:], in_=fj.rearrange("(p r) o -> p (r o)", r=PACK))
         nc.sync.dma_start(out=x_w[:].bitcast(I32), in_=xt_words.rearrange("z p c -> p z c").bitcast(I32))
-        nc.sync.dma_start(out=ws_w[:], in_=ws_words.rearrange("z p c r -> p z (c r)").bitcast(I32))
-        for q in range(2, QUADS):
-            load_scale_rows(nc.sync, x_s, xt_scales, q)
         for q in range(QUADS):
+            load_scale_rows(nc.sync, x_s, xt_scales, q)
+        load_scale_rows(nc.sync, ws_s, ws_scales, 0)
+        nc.sync.dma_start(out=ws_w[:], in_=ws_words.rearrange("z p c r -> p z (c r)").bitcast(I32))
+        for q in range(1, QUADS):
             load_scale_rows(nc.sync, ws_s, ws_scales, q)
         nc.sync.dma_start(out=wy_w_in[:], in_=wy_words.rearrange("z p c r -> p z (c r)").bitcast(I32))
-        nc.sync.dma_start(out=fj_col[:], in_=fj.rearrange("(p r) o -> p (r o)", r=PACK))
         for q in range(QUADS):
             load_scale_rows(nc.sync, wy_s_in, wy_scales, q)
         nc.sync.dma_start(out=wo_w_in[:].bitcast(I32), in_=wo_words[0].bitcast(I32))
@@ -109,6 +112,14 @@ def tile_mix_shares_carry_slot_rows_pl_kernel(
             for r in range(PACK):
                 nc.tensor.transpose(
                     fj_rows[:, r // 2, :, r % 2], fj_col[:, r : r + 1].to_broadcast([P, P]), ident[:]
+                )
+
+        def warm_up():
+            unread = bank(6, "unread", [P, P])
+            for n in range(WARM_UP_PASSES):
+                nc.tensor.matmul_mx(
+                    out=unread[:], lhsT=zero_codes[:].bitcast(FP8X4), lhsT_scale=zero_plane[:],
+                    rhs=x_codes(0, 0), rhs_scale=zero_plane[:], start=True, stop=True,
                 )
 
         def row_max(i):
@@ -152,30 +163,31 @@ def tile_mix_shares_carry_slot_rows_pl_kernel(
             q_plane[i] = sbuf("q_plane%d" % i, [P, P], U8)
             nc.vector.quantize_mx(out=q_codes[i][:].bitcast(FP8X4), scales=q_plane[i][:], in_=grouped[i][:])
 
-        def deal_wy_words(z):
+        def deal_wy_words():
             nc.vector.tensor_copy(
-                out=wy_w[z][:].rearrange("p r (b m) -> p b r m", m=4),
-                in_=wy_w_in[:, z, :].rearrange("p (b m r) -> p b r m", m=4, r=PACK),
+                out=wy_w[:].rearrange("p z r (b m) -> p z b r m", m=4),
+                in_=wy_w_in[:].rearrange("p z (b m r) -> p z b r m", m=4, r=PACK),
             )
 
         def deal_wy_scales():
-            nc.vector.tensor_copy(out=wy_s[:], in_=wy_s_in[:].rearrange("p z (m r) -> p z r m", r=PACK))
+            for z in range(PASSES):
+                nc.gpsimd.tensor_copy(out=wy_s[z][:], in_=wy_s_in[:, z, :].rearrange("p (m r) -> p r m", r=PACK))
 
         def deal_wo_words():
-            nc.vector.tensor_copy(
-                out=wo_w[:].rearrange("p r (b m h) -> p b r m h", m=8, h=2),
-                in_=wo_w_in[:].rearrange("p (b m r h) -> p b r m h", m=8, r=PACK, h=2),
-            )
+            dealt = wo_w[:].rearrange("p r (b m h) -> p b r m h", m=8, h=2)
+            raw = wo_w_in[:].rearrange("p (b m r h) -> p b r m h", m=8, r=PACK, h=2)
+            for half in (slice(0, 8), slice(8, 16)):
+                nc.gpsimd.tensor_copy(out=dealt[:, half], in_=raw[:, half])
 
         def deal_wo_scales():
-            nc.vector.tensor_copy(out=wo_s[:], in_=wo_s_in[:, 0, :].rearrange("p (m r) -> p r m", r=PACK))
+            nc.gpsimd.tensor_copy(out=wo_s[:], in_=wo_s_in[:, 0, :].rearrange("p (m r) -> p r m", r=PACK))
 
         def own_product(i):
             y[i] = bank((4, 5, 6, 2)[i], "y%d" % i, [P, PACK, P])
             for z in range(PASSES):
                 for r in range(PACK):
                     nc.tensor.matmul_mx(
-                        out=y[i][:, r, :], lhsT=wy_w[z][:, r, :].bitcast(FP8X4), lhsT_scale=wy_s[:, z, r, :],
+                        out=y[i][:, r, :], lhsT=wy_w[:, z, r, :].bitcast(FP8X4), lhsT_scale=wy_s[z][:, r, :],
                         rhs=x_codes(z, i), rhs_scale=x_plane(z, i),
                         start=(z == 0 and r == 0), stop=False,
                     )
@@ -214,18 +226,20 @@ def tile_mix_shares_carry_slot_rows_pl_kernel(
                     in_=y_codes[:, both].bitcast(I32),
                 )
 
+        spread_fj()
+        warm_up()
         scores(0)
         scores(1)
         scores(2)
-        spread_fj()
         scores(3)
-        deal_wy_words(0)
+        deal_wy_scales()
+        deal_wo_words()
+        deal_wo_scales()
         row_max(0)
         exponentials(0)
-        deal_wy_words(1)
+        deal_wy_words()
         row_max(1)
         exponentials(1)
-        deal_wy_scales()
         own_product(0)
         own_product(1)
         reciprocal(0)
@@ -236,41 +250,39 @@ def tile_mix_shares_carry_slot_rows_pl_kernel(
         own_product(2)
         reciprocal(1)
         row_max(3)
-        exponentials(3)
         group(0)
+        exponentials(3)
         weigh(1)
         turn(1)
         group(1)
-        own_product(3)
         reciprocal(2)
-        deal_wo_scales()
+        quantise_shares(0)
+        carry(0)
         weigh(2)
         turn(2)
-        group(2)
+        own_product(3)
         reciprocal(3)
-        quantise_shares(0)
         weigh(3)
-        turn(3)
-        group(3)
-        deal_wo_words()
-        carry(0)
         quantise_shares(1)
+        turn(3)
         carry(1)
+        hand_out_values(0, nc.scalar.copy)
+        group(2)
+        group(3)
+        round_on_vector(0)
         quantise_shares(2)
         carry(2)
-        hand_out_values(0, nc.scalar.copy)
         quantise_shares(3)
         carry(3)
-        hand_out_values(1, nc.vector.tensor_copy)
-        hand_out_values(2, nc.scalar.copy)
-        round_on_vector(0)
+        hand_out_values(1, nc.scalar.copy)
+        hand_out_codes(0)
+        hand_out_values(2, nc.vector.tensor_copy)
         round_on_vector(1)
         hand_out_values(3, nc.scalar.copy)
-        hand_out_codes(0)
         round_on_vector(2)
         hand_out_codes(1)
-        round_on_vector(3)
         hand_out_codes(2)
+        round_on_vector(3)
         hand_out_codes(3)
         for q in range(QUADS):
             engine = nc.sync if q % 2 else nc.scalar

@@ -69,24 +69,31 @@ def tile_mix_shares_carry_slot_rows_pl_kernel(
         zeros = sbuf("zeros", [P, PACK * P], BF16)
         zero_codes = sbuf("zero_codes", [P, P], U32)
         zero_plane = sbuf("zero_plane", [P, P], U8)
-        for blank in (ws_s, zeros, wy_s_in, wo_s_in):
+        for blank in (wy_s_in, ws_s, zeros, wo_s_in):
             nc.vector.memset(blank[:].bitcast(I32), 0)
         nc.vector.quantize_mx(out=zero_codes[:].bitcast(FP8X4), scales=zero_plane[:], in_=zeros[:])
 
+        load_scale_rows(nc.gpsimd, wy_s_in, wy_scales, 3)
         nc.sync.dma_start(out=fj_col[:], in_=fj.rearrange("(p r) o -> p (r o)", r=PACK))
         nc.sync.dma_start(out=x_w[:].bitcast(I32), in_=xt_words.rearrange("z p c -> p z c").bitcast(I32))
-        for q in range(QUADS):
-            load_scale_rows(nc.sync, x_s, xt_scales, q)
+        load_scale_rows(nc.sync, x_s, xt_scales, 0)
+        load_scale_rows(nc.sync, x_s, xt_scales, 1)
+        load_scale_rows(nc.sync, x_s, xt_scales, 2)
+        load_scale_rows(nc.sync, x_s, xt_scales, 3)
         load_scale_rows(nc.sync, ws_s, ws_scales, 0)
         nc.sync.dma_start(out=ws_w[:], in_=ws_words.rearrange("z p c r -> p z (c r)").bitcast(I32))
-        for q in range(1, QUADS):
-            load_scale_rows(nc.sync, ws_s, ws_scales, q)
+        load_scale_rows(nc.sync, ws_s, ws_scales, 1)
+        load_scale_rows(nc.sync, ws_s, ws_scales, 2)
+        load_scale_rows(nc.sync, ws_s, ws_scales, 3)
+        load_scale_rows(nc.sync, wy_s_in, wy_scales, 0)
+        load_scale_rows(nc.sync, wy_s_in, wy_scales, 1)
+        load_scale_rows(nc.sync, wy_s_in, wy_scales, 2)
         nc.sync.dma_start(out=wy_w_in[:], in_=wy_words.rearrange("z p c r -> p z (c r)").bitcast(I32))
-        for q in range(QUADS):
-            load_scale_rows(nc.sync, wy_s_in, wy_scales, q)
+        load_scale_rows(nc.sync, wo_s_in, wo_scales, 0)
+        load_scale_rows(nc.sync, wo_s_in, wo_scales, 1)
+        load_scale_rows(nc.sync, wo_s_in, wo_scales, 2)
+        load_scale_rows(nc.sync, wo_s_in, wo_scales, 3)
         nc.sync.dma_start(out=wo_w_in[:].bitcast(I32), in_=wo_words[0].bitcast(I32))
-        for q in range(QUADS):
-            load_scale_rows(nc.sync, wo_s_in, wo_scales, q)
 
         def x_codes(z, i):
             return x_w[:, z, 2 * P * i : 2 * P * (i + 1)].bitcast(FP4X4)
@@ -237,52 +244,52 @@ def tile_mix_shares_carry_slot_rows_pl_kernel(
         deal_wo_scales()
         row_max(0)
         exponentials(0)
-        deal_wy_words()
         row_max(1)
         exponentials(1)
+        deal_wy_words()
         own_product(0)
         own_product(1)
-        reciprocal(0)
+        own_product(2)
         row_max(2)
         exponentials(2)
-        weigh(0)
-        turn(0)
-        own_product(2)
+        reciprocal(0)
         reciprocal(1)
         row_max(3)
-        group(0)
         exponentials(3)
+        weigh(0)
+        turn(0)
+        group(0)
+        reciprocal(2)
         weigh(1)
         turn(1)
         group(1)
-        reciprocal(2)
-        quantise_shares(0)
-        carry(0)
-        weigh(2)
-        turn(2)
         own_product(3)
         reciprocal(3)
+        weigh(2)
+        turn(2)
+        quantise_shares(0)
+        carry(0)
         weigh(3)
-        quantise_shares(1)
         turn(3)
-        carry(1)
-        hand_out_values(0, nc.scalar.copy)
         group(2)
-        group(3)
-        round_on_vector(0)
+        quantise_shares(1)
+        carry(1)
         quantise_shares(2)
         carry(2)
+        group(3)
+        hand_out_values(0, nc.vector.tensor_copy)
         quantise_shares(3)
         carry(3)
         hand_out_values(1, nc.scalar.copy)
-        hand_out_codes(0)
-        hand_out_values(2, nc.vector.tensor_copy)
+        round_on_vector(0)
+        hand_out_values(2, nc.scalar.copy)
         round_on_vector(1)
+        hand_out_codes(0)
         hand_out_values(3, nc.scalar.copy)
-        round_on_vector(2)
         hand_out_codes(1)
-        hand_out_codes(2)
+        round_on_vector(2)
         round_on_vector(3)
+        hand_out_codes(2)
         hand_out_codes(3)
         for q in range(QUADS):
             engine = nc.sync if q % 2 else nc.scalar

from contextlib import ExitStack

import concourse.mybir as mybir
from concourse.masks import make_identity

K, T, J, N = 1024, 512, 512, 512
FLOPS = 2 * K * T * J + 2 * J * N * T + 2 * K * N * T

F32 = mybir.dt.float32
BF16 = mybir.dt.bfloat16
I32 = mybir.dt.int32
U32 = mybir.dt.uint32
U8 = mybir.dt.uint8
FP8X4 = mybir.dt.float8_e4m3fn_x4
FP4X4 = mybir.dt.float4_e2m1fn_x4
ALU = mybir.AluOpType
ACT = mybir.ActivationFunctionType
AX = mybir.AxisListType

P = 128
PACK = 4
PASSES = K // (P * PACK)
TILES = T // P
QUADS = 4
WARM_UP_PASSES = 12


def tile_mix_shares_carry_slot_rows_pl_kernel(
    tc, xt_words, xt_scales, ws_words, ws_scales, fj, wo_words, wo_scales, wy_words, wy_scales,
    out_0, out_1, out_2,
):
    nc = tc.nc
    with ExitStack() as ctx:
        sb = ctx.enter_context(tc.tile_pool(name="sb", bufs=1))
        ps = ctx.enter_context(tc.psum_pool(name="ps", bufs=1))
        ctx.enter_context(tc.manual_schedule())

        def sbuf(name, shape, dtype):
            return sb.tile(shape, dtype, name=name, align_bytes=64)

        def bank(number, name, shape):
            return ps.tile(shape, F32, name=name, tag="bank%d" % number)

        x_w = sbuf("x_w", [P, PASSES, 2 * T], U8)
        x_s = sbuf("x_s", [P, PASSES, T], U8)
        ws_w = sbuf("ws_w", [P, PASSES, J], I32)
        ws_s = sbuf("ws_s", [P, PASSES, J], U8)
        wy_w_in = sbuf("wy_w_in", [P, PASSES, N], I32)
        wy_s_in = sbuf("wy_s_in", [P, PASSES, N], U8)
        wo_w_in = sbuf("wo_w_in", [P, 2 * N], U8)
        wo_s_in = sbuf("wo_s_in", [P, 1, N], U8)
        wy_w = sbuf("wy_w", [P, PASSES, PACK, P], I32)
        wy_s = [sbuf("wy_s%d" % z, [P, PACK, P], U8) for z in range(PASSES)]
        wo_w = sbuf("wo_w", [P, PACK, 2 * P], U8)
        wo_s = sbuf("wo_s", [P, PACK, P], U8)
        fj_col = sbuf("fj_col", [P, PACK], F32)
        ident = sbuf("ident", [P, P], F32)
        y_scales = sbuf("y_scales", [P, T], U8)
        y_codes = sbuf("y_codes", [P, T], U32)

        def load_scale_rows(engine, plane, rows, q):
            engine.dma_start(
                out=plane[32 * q : 32 * q + 4].bitcast(I32),
                in_=rows[:, 4 * q : 4 * q + 4, :].rearrange("z r c -> r z c").bitcast(I32),
            )

        nc.gpsimd.memset(x_s[:].bitcast(I32), 0)
        make_identity(nc, ident[:])
        zeros = sbuf("zeros", [P, PACK * P], BF16)
        zero_codes = sbuf("zero_codes", [P, P], U32)
        zero_plane = sbuf("zero_plane", [P, P], U8)
        for blank in (wy_s_in, ws_s, zeros, wo_s_in):
            nc.vector.memset(blank[:].bitcast(I32), 0)
        nc.vector.quantize_mx(out=zero_codes[:].bitcast(FP8X4), scales=zero_plane[:], in_=zeros[:])

        load_scale_rows(nc.gpsimd, wy_s_in, wy_scales, 3)
        nc.sync.dma_start(out=fj_col[:], in_=fj.rearrange("(p r) o -> p (r o)", r=PACK))
        nc.sync.dma_start(out=x_w[:].bitcast(I32), in_=xt_words.rearrange("z p c -> p z c").bitcast(I32))
        load_scale_rows(nc.sync, x_s, xt_scales, 0)
        load_scale_rows(nc.sync, x_s, xt_scales, 1)
        load_scale_rows(nc.sync, x_s, xt_scales, 2)
        load_scale_rows(nc.sync, x_s, xt_scales, 3)
        load_scale_rows(nc.sync, ws_s, ws_scales, 0)
        nc.sync.dma_start(out=ws_w[:], in_=ws_words.rearrange("z p c r -> p z (c r)").bitcast(I32))
        load_scale_rows(nc.sync, ws_s, ws_scales, 1)
        load_scale_rows(nc.sync, ws_s, ws_scales, 2)
        load_scale_rows(nc.sync, ws_s, ws_scales, 3)
        load_scale_rows(nc.sync, wy_s_in, wy_scales, 0)
        load_scale_rows(nc.sync, wy_s_in, wy_scales, 1)
        load_scale_rows(nc.sync, wy_s_in, wy_scales, 2)
        nc.sync.dma_start(out=wy_w_in[:], in_=wy_words.rearrange("z p c r -> p z (c r)").bitcast(I32))
        load_scale_rows(nc.sync, wo_s_in, wo_scales, 0)
        load_scale_rows(nc.sync, wo_s_in, wo_scales, 1)
        load_scale_rows(nc.sync, wo_s_in, wo_scales, 2)
        load_scale_rows(nc.sync, wo_s_in, wo_scales, 3)
        nc.sync.dma_start(out=wo_w_in[:].bitcast(I32), in_=wo_words[0].bitcast(I32))

        def x_codes(z, i):
            return x_w[:, z, 2 * P * i : 2 * P * (i + 1)].bitcast(FP4X4)

        def x_plane(z, i):
            return x_s[:, z, P * i : P * (i + 1)]

        score, neg_max, e, total, inv, qw, turned, grouped, q_codes, q_plane = ({} for n in range(10))
        y, y_f32, y_bf = {}, {}, {}

        def scores(i):
            score[i] = bank(i, "score%d" % i, [P, J])
            for z in range(PASSES):
                nc.tensor.matmul_mx(
                    out=score[i][:], lhsT=x_codes(z, i), lhsT_scale=x_plane(z, i),
                    rhs=ws_w[:, z, :].bitcast(FP8X4), rhs_scale=ws_s[:, z, :],
                    start=(z == 0), stop=(z == PASSES - 1),
                )

        fj_rows = bank(7, "fj_rows", [P, 2, P, 2])

        def spread_fj():
            for r in range(PACK):
                nc.tensor.transpose(
                    fj_rows[:, r // 2, :, r % 2], fj_col[:, r : r + 1].to_broadcast([P, P]), ident[:]
                )

        def warm_up():
            unread = bank(6, "unread", [P, P])
            for n in range(WARM_UP_PASSES):
                nc.tensor.matmul_mx(
                    out=unread[:], lhsT=zero_codes[:].bitcast(FP8X4), lhsT_scale=zero_plane[:],
                    rhs=x_codes(0, 0), rhs_scale=zero_plane[:], start=True, stop=True,
                )

        def row_max(i):
            neg_max[i] = sbuf("neg_max%d" % i, [P, 1], F32)
            nc.vector.tensor_reduce(out=neg_max[i][:], in_=score[i][:], axis=AX.X, op=ALU.max, negate=True)

        def exponentials(i):
            e[i] = sbuf("e%d" % i, [P, 2, P, 2], F32)
            total[i] = sbuf("total%d" % i, [P, 1], F32)
            nc.scalar.activation(
                out=e[i][:], in_=score[i][:].rearrange("p (m u v) -> p u m v", u=2, v=2),
                func=ACT.Exp, bias=neg_max[i][:], scale=1.0, accum_out=total[i][:],
            )

        def reciprocal(i):
            inv[i] = sbuf("inv%d" % i, [P, 1], F32)
            nc.vector.reciprocal(out=inv[i][:], in_=total[i][:])

        def weigh(i):
            qw[i] = sbuf("qw%d" % i, [P, J], BF16)
            nc.vector.scalar_tensor_tensor(
                out=qw[i][:], in0=e[i][:].rearrange("p u m v -> p (u m v)"), scalar=inv[i][:],
                in1=fj_rows[:].rearrange("p u m v -> p (u m v)"), op0=ALU.mult, op1=ALU.mult,
            )

        def turn(i):
            turned[i] = bank(i % 2, "turned%d" % i, [P, 2, P])
            pairs = qw[i][:].bitcast(F32)
            for u in range(2):
                nc.tensor.transpose(turned[i][:, u, :], pairs[:, P * u : P * (u + 1)], ident[:])

        def group(i):
            grouped[i] = sbuf("grouped%d" % i, [P, PACK * P], BF16)
            nc.scalar.copy(
                out=grouped[i][:].bitcast(F32).rearrange("p (t u) -> p t u", u=2),
                in_=turned[i][:].rearrange("p u t -> p t u"),
            )

        def quantise_shares(i):
            q_codes[i] = sbuf("q_codes%d" % i, [P, P], U32)
            q_plane[i] = sbuf("q_plane%d" % i, [P, P], U8)
            nc.vector.quantize_mx(out=q_codes[i][:].bitcast(FP8X4), scales=q_plane[i][:], in_=grouped[i][:])

        def deal_wy_words():
            nc.vector.tensor_copy(
                out=wy_w[:].rearrange("p z r (b m) -> p z b r m", m=4),
                in_=wy_w_in[:].rearrange("p z (b m r) -> p z b r m", m=4, r=PACK),
            )

        def deal_wy_scales():
            for z in range(PASSES):
                nc.gpsimd.tensor_copy(out=wy_s[z][:], in_=wy_s_in[:, z, :].rearrange("p (m r) -> p r m", r=PACK))

        def deal_wo_words():
            dealt = wo_w[:].rearrange("p r (b m h) -> p b r m h", m=8, h=2)
            raw = wo_w_in[:].rearrange("p (b m r h) -> p b r m h", m=8, r=PACK, h=2)
            for half in (slice(0, 8), slice(8, 16)):
                nc.gpsimd.tensor_copy(out=dealt[:, half], in_=raw[:, half])

        def deal_wo_scales():
            nc.gpsimd.tensor_copy(out=wo_s[:], in_=wo_s_in[:, 0, :].rearrange("p (m r) -> p r m", r=PACK))

        def own_product(i):
            y[i] = bank((4, 5, 6, 2)[i], "y%d" % i, [P, PACK, P])
            for z in range(PASSES):
                for r in range(PACK):
                    nc.tensor.matmul_mx(
                        out=y[i][:, r, :], lhsT=wy_w[:, z, r, :].bitcast(FP8X4), lhsT_scale=wy_s[z][:, r, :],
                        rhs=x_codes(z, i), rhs_scale=x_plane(z, i),
                        start=(z == 0 and r == 0), stop=False,
                    )

        def carry(i):
            for r in range(PACK):
                nc.tensor.matmul_mx(
                    out=y[i][:, r, :], lhsT=wo_w[:, r, :].bitcast(FP4X4), lhsT_scale=wo_s[:, r, :],
                    rhs=q_codes[i][:].bitcast(FP8X4), rhs_scale=q_plane[i][:],
                    start=False, stop=(r == PACK - 1),
                )

        def hand_out_values(i, copy):
            y_f32[i] = sbuf("y_f32_%d" % i, [P, PACK, P], F32)
            copy(out=y_f32[i][:], in_=y[i][:])
            nc.sync.dma_start(
                out=out_0.rearrange("(p r) t -> p r t", r=PACK)[:, :, P * i : P * (i + 1)], in_=y_f32[i][:]
            )

        def round_on_vector(i):
            y_bf[i] = sbuf("y_bf%d" % i, [P, P, PACK], BF16)
            nc.vector.tensor_copy(
                out=y_bf[i][:].rearrange("p (c m) r -> p c r m", m=4),
                in_=y_f32[i][:].rearrange("p r (c m) -> p c r m", m=4),
            )

        def hand_out_codes(i):
            nc.vector.quantize_mx(
                out=y_codes[:, P * i : P * (i + 1)].bitcast(FP8X4), scales=y_scales[:, P * i : P * (i + 1)],
                in_=y_bf[i][:].rearrange("p t r -> p (t r)"),
            )
            if i % 2:
                both = slice(P * (i - 1), P * (i + 1))
                nc.sync.dma_start(
                    out=out_1[0].rearrange("p c r -> p (c r)").bitcast(I32)[:, both],
                    in_=y_codes[:, both].bitcast(I32),
                )

        spread_fj()
        warm_up()
        scores(0)
        scores(1)
        scores(2)
        scores(3)
        deal_wy_scales()
        deal_wo_words()
        deal_wo_scales()
        row_max(0)
        exponentials(0)
        row_max(1)
        exponentials(1)
        deal_wy_words()
        own_product(0)
        own_product(1)
        own_product(2)
        row_max(2)
        exponentials(2)
        reciprocal(0)
        reciprocal(1)
        row_max(3)
        exponentials(3)
        weigh(0)
        turn(0)
        group(0)
        reciprocal(2)
        weigh(1)
        turn(1)
        group(1)
        own_product(3)
        reciprocal(3)
        weigh(2)
        turn(2)
        quantise_shares(0)
        carry(0)
        weigh(3)
        turn(3)
        group(2)
        quantise_shares(1)
        carry(1)
        quantise_shares(2)
        carry(2)
        group(3)
        hand_out_values(0, nc.vector.tensor_copy)
        quantise_shares(3)
        carry(3)
        hand_out_values(1, nc.scalar.copy)
        round_on_vector(0)
        hand_out_values(2, nc.scalar.copy)
        round_on_vector(1)
        hand_out_codes(0)
        hand_out_values(3, nc.scalar.copy)
        hand_out_codes(1)
        round_on_vector(2)
        round_on_vector(3)
        hand_out_codes(2)
        hand_out_codes(3)
        for q in range(QUADS):
            engine = nc.sync if q % 2 else nc.scalar
            engine.dma_start(
                out=out_2[0, 4 * q : 4 * q + 4, :].bitcast(I32),
                in_=y_scales[32 * q : 32 * q + 4, :].bitcast(I32),
            )
